import numpy as np
import ml_dtypes


def mxq(x, axis, fmt="e4m3"):
    dtype, down = {"e4m3": (ml_dtypes.float8_e4m3fn, 7), "e5m2": (ml_dtypes.float8_e5m2, 14)}[fmt]
    v = np.moveaxis(np.asarray(x, np.float32).astype(ml_dtypes.bfloat16).astype(np.float64), axis, -1)
    blocks = v.reshape(v.shape[:-1] + (-1, 32))
    amax = np.abs(blocks).max(-1, keepdims=True)
    byte = np.maximum(np.where(amax > 0, np.frexp(amax)[1] - 1 + 127, 0) - down, 1)
    scale = np.exp2(byte - 127.0)
    codes = (blocks / scale).astype(np.float32).astype(dtype).astype(np.float64)
    return np.moveaxis((codes * scale).reshape(v.shape), -1, axis)


WIDE = False


def mx_kscale(k):
    if not WIDE:
        return np.ones(k)
    levels = np.array([10, -10, 5, -5, 0])
    if k % 512:
        return np.exp2(np.random.permutation(np.resize(levels, k // 32))).repeat(32)
    a = np.empty((k // 512, 16))
    for p in range(k // 512):
        a[p, :8] = np.random.permutation(np.resize(levels, 8))
        for g in range(8):
            far = levels[np.abs(levels - a[p, g]) >= 10]
            a[p, g + 8] = far[np.random.randint(len(far))]
    return np.exp2(a.ravel()).repeat(32)


def f64(x):
    return np.asarray(x).astype(np.float64)


def striped(idx):
    return np.tile(idx.reshape(-1, 16).T, (8, 1)).astype(np.uint16)


def unstriped(offs):
    return offs[:16].T.reshape(-1).astype(np.int64)


E2M1 = np.array([0.0, 0.5, 1.0, 1.5, 2.0, 3.0, 4.0, 6.0, -0.0, -0.5, -1.0, -1.5, -2.0, -3.0, -4.0, -6.0])


def pack_weight(w, fmt):
    k, n = w.shape
    w = f64(np.asarray(w, np.float32).astype(ml_dtypes.bfloat16)).reshape(k // 32, 32, n)
    amax = np.abs(w).max(1)
    if fmt == "e4m3":
        byte = np.frexp(amax)[1] - 1 + 127 - 7
    else:
        mant, ex = np.frexp(amax / 6.0)
        byte = np.where(mant > 0.5, ex, ex - 1) + 127
    byte = np.clip(np.where(amax > 0, byte, 1), 1, 254)
    scaled = (w * np.exp2(127.0 - byte)[:, None, :]).reshape(k, n).astype(np.float32)
    by_word = np.ascontiguousarray(scaled.reshape(k // 512, 128, 4, n).transpose(0, 1, 3, 2))
    if fmt == "e4m3":
        words = by_word.astype(ml_dtypes.float8_e4m3fn).view(np.uint8)
    else:
        c = by_word.astype(ml_dtypes.float4_e2m1fn).view(np.uint8) & 0xF
        words = (c[..., 0::2] | (c[..., 1::2] << 4)).reshape(k // 512, 128, 2 * n)
    return np.ascontiguousarray(words), np.ascontiguousarray(byte.astype(np.uint8).reshape(k // 512, 16, n))


def unpack_weight(words, scales, fmt):
    g, _, n = scales.shape
    words = np.ascontiguousarray(words).reshape(g, 128, n, -1)
    if fmt == "e4m3":
        vals = words.view(ml_dtypes.float8_e4m3fn).astype(np.float64)
    else:
        nib = np.empty((g, 128, n, 4), np.uint8)
        nib[..., 0::2] = words & 0xF
        nib[..., 1::2] = words >> 4
        vals = E2M1[nib]
    vals = vals * np.repeat(np.exp2(scales.astype(np.float64) - 127.0), 8, axis=1)[..., None]
    return vals.transpose(0, 1, 3, 2).reshape(g * 512, n)


def gelu(v):
    return 0.5 * v * (1.0 + np.tanh(np.sqrt(2.0 / np.pi) * (v + 0.044715 * v**3)))


K, K2, H, N, T, S = 1536, 512, 1024, 384, 4096, 1024

def setup_inputs():
    n = np.random.standard_normal
    s = mx_kscale(K)[:, None]
    s2 = mx_kscale(K2)[:, None]
    u = mx_kscale(H)[:, None]
    d = {}
    d["tab_words"], d["tab_scales"] = pack_weight(n((K, T)) * s, "e4m3")
    d["offs"] = striped(np.random.permutation(T)[:S])
    d["xs_words"], d["xs_scales"] = pack_weight(n((K2, S)) * s2, "e4m3")
    d["wa"] = (0.6 * n((K, H)) / s / K ** 0.5).astype(np.float32)
    d["wb_words"], d["wb_scales"] = pack_weight(0.6 * n((K2, H)) / s2 / K2 ** 0.5, "e2m1")
    d["lag"] = (0.5 * n(H)).astype(np.float32)
    d["trust"] = (np.exp(0.4 * n((H, S))) * u).astype(np.float32)
    d["wo"] = (0.7 * n((H, N)) / u / H ** 0.5).astype(np.float32)
    d["level"] = (0.5 * n(N)).astype(np.float32)
    return d

def reference(tab_words, tab_scales, offs, xs_words, xs_scales, wa, wb_words, wb_scales, lag, trust, wo, level):
    v = unpack_weight(tab_words, tab_scales, "e4m3")[:, unstriped(offs)]
    xs = unpack_weight(xs_words, xs_scales, "e4m3")
    wb = unpack_weight(wb_words, wb_scales, "e2m1")
    lot = mxq(f64(wa), 0, "e4m3").T @ v
    probe = wb.T @ xs
    dev = lot - probe - f64(lag)[:, None]
    h = np.square(dev) * f64(trust)
    y = mxq(f64(wo), 0, "e4m3").T @ mxq(h, 0, "e4m3")
    return np.tanh(y + f64(level)[:, None])

@@ -1,0 +1,284 @@
+from contextlib import ExitStack
+
+import concourse.mybir as mybir
+
+K, K2, H, N, T, S = 1536, 512, 1024, 384, 4096, 1024
+FLOPS = 2 * S * (K * H + K2 * H + H * N)
+
+F32 = mybir.dt.float32
+BF16 = mybir.dt.bfloat16
+I32 = mybir.dt.int32
+U32 = mybir.dt.uint32
+U16 = mybir.dt.uint16
+U8 = mybir.dt.uint8
+FP8X4 = mybir.dt.float8_e4m3fn_x4
+FP4X4 = mybir.dt.float4_e2m1fn_x4
+ACT = mybir.ActivationFunctionType
+MULT = mybir.AluOpType.mult
+
+P = 128
+PACK = 4
+PASS = P * PACK
+BANK = 512
+K_PASSES = K // PASS
+R_PASSES = H // PASS
+HALVES = S // BANK
+N_TILES = N // P
+
+
+def tile_list_drum_curve_deviation_kernel(
+    tc, tab_words, tab_scales, offs, xs_words, xs_scales, wa, wb_words, wb_scales, lag, trust, wo, level, out
+):
+    nc = tc.nc
+    with ExitStack() as ctx:
+        keep = ctx.enter_context(tc.tile_pool(name="keep", bufs=1))
+        ring = ctx.enter_context(tc.tile_pool(name="ring", bufs=2))
+        psum = ctx.enter_context(tc.psum_pool(name="psum", bufs=8))
+
+        def held(shape, dtype, name):
+            return keep.tile(shape, dtype, name=name, align_bytes=64)
+
+        offsets = keep.tile([P, S // 16], U16, name="offsets")
+        tab_sc = held([P, T], U8, "tab_sc")
+        wb_sc_raw = held([P, H], U8, "wb_sc_raw")
+        xs_sc = held([P, S], U8, "xs_sc")
+        lag_sb = [held([P, PACK], F32, "lag_sb_%d" % b) for b in range(R_PASSES)]
+        level_sb = held([P, N_TILES], F32, "level_sb")
+
+        nc.gpsimd.memset(tab_sc[:].bitcast(I32), 0)
+        for plane in (wb_sc_raw, xs_sc):
+            nc.vector.memset(plane[:].bitcast(I32), 0)
+
+        def load_table_scales(q):
+            nc.sync.dma_start(
+                out=tab_sc[32 * q : 32 * q + 4 * K_PASSES, :].bitcast(I32),
+                in_=tab_scales[:, 4 * q : 4 * q + 4, :].bitcast(I32),
+            )
+
+        def load_scale_rows(plane, rows, q):
+            nc.sync.dma_start(
+                out=plane[32 * q : 32 * q + 4, :].bitcast(I32),
+                in_=rows[0, 4 * q : 4 * q + 4, :].bitcast(I32),
+            )
+
+        tab_sb, wa_raw, trust_sb, wo_raw = {}, {}, {}, {}
+
+        def load_tab(a):
+            tab_sb[a] = held([P, T], U32, "tab_%d" % a)
+            nc.sync.dma_start(
+                out=tab_sb[a][:].bitcast(I32), in_=tab_words[a].rearrange("p n i -> p (n i)").bitcast(I32)
+            )
+
+        def wide_tile(name):
+            return ring.tile([P, PACK, BANK], F32, name=name, tag="wide", bufs=K_PASSES * R_PASSES)
+
+        def load_wa(a, b):
+            wa_raw[a, b] = wide_tile("wa_raw_%d_%d" % (a, b))
+            rows = wa[PASS * a : PASS * (a + 1), PASS * b : PASS * (b + 1)]
+            nc.sync.dma_start(out=wa_raw[a, b][:], in_=rows.rearrange("(p i) r -> p i r", i=PACK))
+
+        def load_trust(b, j0, width):
+            trust_sb[b, j0] = held([P, PACK, width], F32, "trust_%d_%d" % (b, j0))
+            rows = trust[PASS * b : PASS * (b + 1), j0 : j0 + width]
+            nc.sync.dma_start(out=trust_sb[b, j0][:], in_=rows.rearrange("(p t) j -> p t j", t=PACK))
+
+        def load_wo(b):
+            wo_raw[b] = held([P, PACK, N], F32, "wo_raw_%d" % b)
+            rows = wo[PASS * b : PASS * (b + 1), :]
+            nc.sync.dma_start(out=wo_raw[b][:], in_=rows.rearrange("(p t) n -> p t n", t=PACK))
+
+        wb_raw = held([P, 2 * H], U8, "wb_raw")
+        xs_sb = held([P, S], U32, "xs_sb")
+
+        nc.sync.dma_start(offsets[:], offs)
+        for b in range(R_PASSES):
+            nc.sync.dma_start(
+                out=lag_sb[b][:], in_=lag[PASS * b : PASS * (b + 1)].rearrange("(p t) -> p t", t=PACK)
+            )
+        with nc.allow_non_contiguous_dma(reason="one bias value a partition"):
+            nc.sync.dma_start(out=level_sb[:], in_=level.rearrange("(c p) -> p c", p=P))
+        nc.sync.dma_start(out=wb_raw[:].bitcast(I32), in_=wb_words[0].bitcast(I32))
+        load_tab(0)
+        nc.sync.dma_start(out=xs_sb[:].bitcast(I32), in_=xs_words[0].rearrange("p n i -> p (n i)").bitcast(I32))
+        load_wa(0, 0)
+        for q in range(4):
+            load_table_scales(q)
+        load_tab(1)
+        for q in range(2):
+            load_scale_rows(wb_sc_raw, wb_scales, q)
+        load_wa(1, 0)
+        for q in range(2, 4):
+            load_scale_rows(wb_sc_raw, wb_scales, q)
+        for q in range(2):
+            load_scale_rows(xs_sc, xs_scales, q)
+        load_wa(2, 0)
+        for q in range(2, 4):
+            load_scale_rows(xs_sc, xs_scales, q)
+        load_tab(2)
+        for a in range(K_PASSES):
+            load_wa(a, 1)
+        load_trust(0, 0, 512)
+        load_trust(1, 0, 512)
+        load_wo(0)
+        load_trust(0, 512, 256)
+        load_wo(1)
+        load_trust(0, 768, 256)
+        load_trust(1, 512, 256)
+        load_trust(1, 768, 256)
+
+        picked, wa_q, acc, squares, wo_q, h_q = {}, {}, {}, {}, {}, {}
+        picked_sc = held([P, S], U8, "picked_sc")
+        wb_q = held([P, 2 * H], U8, "wb_q")
+        wb_sc = held([P, H], U8, "wb_sc")
+
+        def gather_words(a):
+            for jh in range(HALVES):
+                picked[a, jh] = held([P, BANK], U32, "picked_%d_%d" % (a, jh))
+                cols = slice(jh * BANK // 16, (jh + 1) * BANK // 16)
+                nc.vector.tensor_copy(picked[a, jh][:], tab_sb[a][:].indirect(offsets[:, cols]))
+
+        def quantize(flat, words, name):
+            codes = held([P, words], U32, name + "_codes")
+            scales = held([P, words], U8, name + "_scales")
+            done = 0
+            while done < words:
+                step = 512 if words - done >= 512 else (256 if words - done >= 256 else 128)
+                nc.vector.quantize_mx(
+                    out=codes[:, done : done + step].bitcast(FP8X4),
+                    scales=scales[:, done : done + step],
+                    in_=flat[:, PACK * done : PACK * (done + step)],
+                )
+                done = done + step
+            return codes, scales
+
+        def quantize_wa(a, b, on_scalar):
+            woven = ring.tile([P, PACK * BANK], BF16, name="wa_woven", align_bytes=64)
+            dst = woven[:].rearrange("p (t m i) -> p m i t", t=PACK, i=PACK)
+            src = wa_raw[a, b][:].rearrange("p i (m t) -> p m i t", t=PACK)
+            if on_scalar:
+                nc.scalar.activation(dst, src, ACT.Copy, scale=-1.0)
+            else:
+                nc.vector.tensor_scalar_mul(dst, src, -1.0)
+            wa_q[a, b] = quantize(woven, BANK, "wa_%d_%d" % (a, b))
+
+        def open_banks(b):
+            for jh in range(HALVES):
+                for t in range(PACK):
+                    acc[b, jh, t] = psum.tile([P, BANK], F32, name="bank")
+
+        def probe_passes(b, start, halves):
+            for jh in halves:
+                for t in range(PACK):
+                    col = PASS * b + P * t
+                    nc.tensor.matmul_mx(
+                        out=acc[b, jh, t][:],
+                        lhsT=wb_q[:, 2 * col : 2 * (col + P)].bitcast(FP4X4),
+                        lhsT_scale=wb_sc[:, col : col + P],
+                        rhs=xs_sb[:, BANK * jh : BANK * (jh + 1)].bitcast(FP8X4),
+                        rhs_scale=xs_sc[:, BANK * jh : BANK * (jh + 1)],
+                        start=start,
+                        stop=False,
+                    )
+
+        def lot_passes(a, b, start, halves):
+            codes, scales = wa_q[a, b]
+            for jh in halves:
+                for t in range(PACK):
+                    nc.tensor.matmul_mx(
+                        out=acc[b, jh, t][:],
+                        lhsT=codes[:, P * t : P * (t + 1)].bitcast(FP8X4),
+                        lhsT_scale=scales[:, P * t : P * (t + 1)],
+                        rhs=picked[a, jh][:].bitcast(FP8X4),
+                        rhs_scale=picked_sc[4 * a : P, BANK * jh : BANK * (jh + 1)],
+                        start=start,
+                        stop=(a == K_PASSES - 1),
+                    )
+
+        def square(b, halves):
+            for jh in halves:
+                squares[b, jh] = wide_tile("squares_%d_%d" % (b, jh))
+                for t in range(PACK):
+                    nc.scalar.activation(
+                        squares[b, jh][:, t, :], acc[b, jh, t][:], ACT.Square, bias=lag_sb[b][:, t : t + 1]
+                    )
+
+        def quantize_h(b, j0, width):
+            woven = ring.tile([P, PACK * BANK], BF16, name="h_woven", align_bytes=64)
+            first = j0 % BANK
+            nc.vector.tensor_tensor(
+                woven[:, : PACK * width].rearrange("p (c i t) -> p c t i", i=4, t=PACK),
+                squares[b, j0 // BANK][:, :, first : first + width].rearrange("p t (c i) -> p c t i", i=4),
+                trust_sb[b, j0][:].rearrange("p t (c i) -> p c t i", i=4),
+                MULT,
+            )
+            h_q[b, j0] = quantize(woven, width, "h_%d_%d" % (b, j0))
+
+        def quantize_wo(b):
+            woven = held([P, PACK * N], BF16, "wo_woven_%d" % b)
+            nc.scalar.copy(
+                woven[:].rearrange("p (c i t) -> p c t i", i=4, t=PACK),
+                wo_raw[b][:].rearrange("p t (c i) -> p c t i", i=4),
+            )
+            wo_q[b] = quantize(woven, N, "wo_%d" % b)
+
+        def readings(j0, width, h_parts):
+            for c in range(N_TILES):
+                bank = psum.tile([P, BANK], F32, name="bank")
+                for b in range(R_PASSES):
+                    w_codes, w_scales = wo_q[b]
+                    (h_codes, h_scales), first = h_parts[b]
+                    nc.tensor.matmul_mx(
+                        out=bank[:, :width],
+                        lhsT=w_codes[:, P * c : P * (c + 1)].bitcast(FP8X4),
+                        lhsT_scale=w_scales[:, P * c : P * (c + 1)],
+                        rhs=h_codes[:, first : first + width].bitcast(FP8X4),
+                        rhs_scale=h_scales[:, first : first + width],
+                        start=(b == 0),
+                        stop=(b == R_PASSES - 1),
+                    )
+                result = held([P, width], F32, "result_%d_%d" % (j0, c))
+                nc.scalar.activation(result[:], bank[:, :width], ACT.Tanh, bias=level_sb[:, c : c + 1])
+                nc.sync.dma_start(out=out[P * c : P * (c + 1), j0 : j0 + width], in_=result[:])
+
+        gather_words(0)
+        nc.vector.tensor_copy(picked_sc[:], tab_sc[:].indirect(offsets[:]))
+        nc.vector.tensor_copy(
+            wb_q[:].rearrange("p (b t m c) -> p b t m c", t=PACK, m=P, c=2),
+            wb_raw[:].rearrange("p (b m t c) -> p b t m c", t=PACK, m=P, c=2),
+        )
+        quantize_wa(0, 0, True)
+        open_banks(0)
+        lot_passes(0, 0, True, (0, 1))
+        gather_words(1)
+        nc.vector.tensor_copy(
+            wb_sc[:].rearrange("p (b t m) -> p b t m", t=PACK, m=P),
+            wb_sc_raw[:].rearrange("p (b m t) -> p b t m", t=PACK, m=P),
+        )
+        quantize_wa(1, 0, True)
+        lot_passes(1, 0, False, (0, 1))
+        probe_passes(0, False, (0, 1))
+        quantize_wa(2, 0, True)
+        gather_words(2)
+        lot_passes(2, 0, False, (0, 1))
+        square(0, (0, 1))
+        open_banks(1)
+        probe_passes(1, True, (0,))
+        for a in range(K_PASSES):
+            quantize_wa(a, 1, False)
+            lot_passes(a, 1, False, (0,))
+        square(1, (0,))
+        probe_passes(1, True, (1,))
+        for a in range(K_PASSES):
+            lot_passes(a, 1, False, (1,))
+        square(1, (1,))
+        quantize_h(0, 0, 512)
+        quantize_h(1, 0, 512)
+        quantize_wo(0)
+        quantize_h(0, 512, 256)
+        quantize_wo(1)
+        readings(0, 512, [(h_q[0, 0], 0), (h_q[1, 0], 0)])
+        quantize_h(0, 768, 256)
+        quantize_h(1, 512, 256)
+        readings(512, 256, [(h_q[0, 512], 0), (h_q[1, 512], 0)])
+        quantize_h(1, 768, 256)
+        readings(768, 256, [(h_q[0, 768], 0), (h_q[1, 768], 0)])

@@ -35,8 +35,8 @@ def tile_list_drum_curve_deviation_kernel(
         ring = ctx.enter_context(tc.tile_pool(name="ring", bufs=2))
         psum = ctx.enter_context(tc.psum_pool(name="psum", bufs=8))
 
-        def held(shape, dtype, name):
-            return keep.tile(shape, dtype, name=name, align_bytes=64)
+        def held(shape, dtype, name, tag=None):
+            return keep.tile(shape, dtype, name=name, tag=tag or name, align_bytes=64)
 
         offsets = keep.tile([P, S // 16], U16, name="offsets")
         tab_sc = held([P, T], U8, "tab_sc")
@@ -69,13 +69,12 @@ def tile_list_drum_curve_deviation_kernel(
                 out=tab_sb[a][:].bitcast(I32), in_=tab_words[a].rearrange("p n i -> p (n i)").bitcast(I32)
             )
 
-        def wide_tile(name):
-            return ring.tile([P, PACK, BANK], F32, name=name, tag="wide", bufs=K_PASSES * R_PASSES)
-
-        def load_wa(a, b):
-            wa_raw[a, b] = wide_tile("wa_raw_%d_%d" % (a, b))
-            rows = wa[PASS * a : PASS * (a + 1), PASS * b : PASS * (b + 1)]
-            nc.sync.dma_start(out=wa_raw[a, b][:], in_=rows.rearrange("(p i) r -> p i r", i=PACK))
+        def load_wa(a, first, count, slot):
+            raw = keep.tile([P, PACK, PASS * count], F32, name="wa_raw_%d_%d" % (a, first), tag="slot_%d" % slot)
+            rows = wa[PASS * a : PASS * (a + 1), PASS * first : PASS * (first + count)]
+            nc.sync.dma_start(out=raw[:], in_=rows.rearrange("(p i) r -> p i r", i=PACK))
+            for b in range(count):
+                wa_raw[a, first + b] = raw[:, :, PASS * b : PASS * (b + 1)]
 
         def load_trust(b, j0, width):
             trust_sb[b, j0] = held([P, PACK, width], F32, "trust_%d_%d" % (b, j0))
@@ -91,6 +90,7 @@ def tile_list_drum_curve_deviation_kernel(
         xs_sb = held([P, S], U32, "xs_sb")
 
         nc.sync.dma_start(offsets[:], offs)
+        load_tab(0)
         for b in range(R_PASSES):
             nc.sync.dma_start(
                 out=lag_sb[b][:], in_=lag[PASS * b : PASS * (b + 1)].rearrange("(p t) -> p t", t=PACK)
@@ -98,35 +98,34 @@ def tile_list_drum_curve_deviation_kernel(
         with nc.allow_non_contiguous_dma(reason="one bias value a partition"):
             nc.sync.dma_start(out=level_sb[:], in_=level.rearrange("(c p) -> p c", p=P))
         nc.sync.dma_start(out=wb_raw[:].bitcast(I32), in_=wb_words[0].bitcast(I32))
-        load_tab(0)
         nc.sync.dma_start(out=xs_sb[:].bitcast(I32), in_=xs_words[0].rearrange("p n i -> p (n i)").bitcast(I32))
-        load_wa(0, 0)
+        load_wa(0, 0, R_PASSES, 0)
         for q in range(4):
             load_table_scales(q)
         load_tab(1)
-        for q in range(2):
+        for q in range(4):
             load_scale_rows(wb_sc_raw, wb_scales, q)
-        load_wa(1, 0)
-        for q in range(2, 4):
-            load_scale_rows(wb_sc_raw, wb_scales, q)
-        for q in range(2):
-            load_scale_rows(xs_sc, xs_scales, q)
-        load_wa(2, 0)
-        for q in range(2, 4):
+        load_wa(1, 0, 1, 1)
+        for q in range(4):
             load_scale_rows(xs_sc, xs_scales, q)
         load_tab(2)
-        for a in range(K_PASSES):
-            load_wa(a, 1)
+        load_wa(2, 0, 1, 2)
+        load_wa(1, 1, 1, 3)
+        load_wa(2, 1, 1, 4)
         load_trust(0, 0, 512)
-        load_trust(1, 0, 512)
         load_wo(0)
-        load_trust(0, 512, 256)
+        load_trust(0, 512, 512)
         load_wo(1)
-        load_trust(0, 768, 256)
-        load_trust(1, 512, 256)
-        load_trust(1, 768, 256)
+        for j0 in range(0, S, 256):
+            load_trust(1, j0, 256)
 
         picked, wa_q, acc, squares, wo_q, h_q = {}, {}, {}, {}, {}, {}
+        for b in range(R_PASSES):
+            for jh in range(HALVES):
+                h_q[b, jh] = (
+                    held([P, BANK], U32, "h_codes_%d_%d" % (b, jh)),
+                    held([P, BANK], U8, "h_scales_%d_%d" % (b, jh)),
+                )
         picked_sc = held([P, S], U8, "picked_sc")
         wb_q = held([P, 2 * H], U8, "wb_q")
         wb_sc = held([P, H], U8, "wb_sc")
@@ -137,8 +136,8 @@ def tile_list_drum_curve_deviation_kernel(
                 cols = slice(jh * BANK // 16, (jh + 1) * BANK // 16)
                 nc.vector.tensor_copy(picked[a, jh][:], tab_sb[a][:].indirect(offsets[:, cols]))
 
-        def quantize(flat, words, name):
-            codes = held([P, words], U32, name + "_codes")
+        def quantize(flat, words, name, tag=None):
+            codes = held([P, words], U32, name + "_codes", tag)
             scales = held([P, words], U8, name + "_scales")
             done = 0
             while done < words:
@@ -154,7 +153,7 @@ def tile_list_drum_curve_deviation_kernel(
         def quantize_wa(a, b, on_scalar):
             woven = ring.tile([P, PACK * BANK], BF16, name="wa_woven", align_bytes=64)
             dst = woven[:].rearrange("p (t m i) -> p m i t", t=PACK, i=PACK)
-            src = wa_raw[a, b][:].rearrange("p i (m t) -> p m i t", t=PACK)
+            src = wa_raw[a, b].rearrange("p i (m t) -> p m i t", t=PACK)
             if on_scalar:
                 nc.scalar.activation(dst, src, ACT.Copy, scale=-1.0)
             else:
@@ -166,9 +165,9 @@ def tile_list_drum_curve_deviation_kernel(
                 for t in range(PACK):
                     acc[b, jh, t] = psum.tile([P, BANK], F32, name="bank")
 
-        def probe_passes(b, start, halves):
+        def probe_passes(b, start, halves, tiles):
             for jh in halves:
-                for t in range(PACK):
+                for t in tiles:
                     col = PASS * b + P * t
                     nc.tensor.matmul_mx(
                         out=acc[b, jh, t][:],
@@ -180,10 +179,10 @@ def tile_list_drum_curve_deviation_kernel(
                         stop=False,
                     )
 
-        def lot_passes(a, b, start, halves):
+        def lot_passes(a, b, start, halves, tiles):
             codes, scales = wa_q[a, b]
             for jh in halves:
-                for t in range(PACK):
+                for t in tiles:
                     nc.tensor.matmul_mx(
                         out=acc[b, jh, t][:],
                         lhsT=codes[:, P * t : P * (t + 1)].bitcast(FP8X4),
@@ -196,7 +195,9 @@ def tile_list_drum_curve_deviation_kernel(
 
         def square(b, halves):
             for jh in halves:
-                squares[b, jh] = wide_tile("squares_%d_%d" % (b, jh))
+                squares[b, jh] = keep.tile(
+                    [P, PACK, BANK], F32, name="squares_%d_%d" % (b, jh), tag="slot_%d" % (HALVES * b + jh)
+                )
                 for t in range(PACK):
                     nc.scalar.activation(
                         squares[b, jh][:, t, :], acc[b, jh, t][:], ACT.Square, bias=lag_sb[b][:, t : t + 1]
@@ -211,22 +212,28 @@ def tile_list_drum_curve_deviation_kernel(
                 trust_sb[b, j0][:].rearrange("p t (c i) -> p c t i", i=4),
                 MULT,
             )
-            h_q[b, j0] = quantize(woven, width, "h_%d_%d" % (b, j0))
+            codes, scales = h_q[b, j0 // BANK]
+            nc.vector.quantize_mx(
+                out=codes[:, first : first + width].bitcast(FP8X4),
+                scales=scales[:, first : first + width],
+                in_=woven[:, : PACK * width],
+            )
 
-        def quantize_wo(b):
+        def quantize_wo(b, after):
             woven = held([P, PACK * N], BF16, "wo_woven_%d" % b)
             nc.scalar.copy(
                 woven[:].rearrange("p (c i t) -> p c t i", i=4, t=PACK),
                 wo_raw[b][:].rearrange("p t (c i) -> p c t i", i=4),
             )
-            wo_q[b] = quantize(woven, N, "wo_%d" % b)
+            wo_q[b] = quantize(woven, N, "wo_%d" % b, "trust_%d_%d" % after)
 
-        def readings(j0, width, h_parts):
+        def readings(j0, width):
+            first = j0 % BANK
             for c in range(N_TILES):
                 bank = psum.tile([P, BANK], F32, name="bank")
                 for b in range(R_PASSES):
                     w_codes, w_scales = wo_q[b]
-                    (h_codes, h_scales), first = h_parts[b]
+                    h_codes, h_scales = h_q[b, j0 // BANK]
                     nc.tensor.matmul_mx(
                         out=bank[:, :width],
                         lhsT=w_codes[:, P * c : P * (c + 1)].bitcast(FP8X4),
@@ -246,39 +253,41 @@ def tile_list_drum_curve_deviation_kernel(
             wb_q[:].rearrange("p (b t m c) -> p b t m c", t=PACK, m=P, c=2),
             wb_raw[:].rearrange("p (b m t c) -> p b t m c", t=PACK, m=P, c=2),
         )
+        every = range(PACK)
         quantize_wa(0, 0, True)
         open_banks(0)
-        lot_passes(0, 0, True, (0, 1))
+        lot_passes(0, 0, True, (0, 1), every)
+        quantize_wa(0, 1, True)
         gather_words(1)
         nc.vector.tensor_copy(
             wb_sc[:].rearrange("p (b t m) -> p b t m", t=PACK, m=P),
             wb_sc_raw[:].rearrange("p (b m t) -> p b t m", t=PACK, m=P),
         )
         quantize_wa(1, 0, True)
-        lot_passes(1, 0, False, (0, 1))
-        probe_passes(0, False, (0, 1))
-        quantize_wa(2, 0, True)
+        lot_passes(1, 0, False, (0, 1), every)
+        probe_passes(0, False, (0, 1), every)
         gather_words(2)
-        lot_passes(2, 0, False, (0, 1))
+        quantize_wa(2, 0, False)
+        lot_passes(2, 0, False, (0, 1), every)
         square(0, (0, 1))
+        quantize_wa(1, 1, False)
+        quantize_wa(2, 1, False)
         open_banks(1)
-        probe_passes(1, True, (0,))
-        for a in range(K_PASSES):
-            quantize_wa(a, 1, False)
-            lot_passes(a, 1, False, (0,))
-        square(1, (0,))
-        probe_passes(1, True, (1,))
-        for a in range(K_PASSES):
-            lot_passes(a, 1, False, (1,))
-        square(1, (1,))
-        quantize_h(0, 0, 512)
-        quantize_h(1, 0, 512)
-        quantize_wo(0)
-        quantize_h(0, 512, 256)
-        quantize_wo(1)
-        readings(0, 512, [(h_q[0, 0], 0), (h_q[1, 0], 0)])
-        quantize_h(0, 768, 256)
+        for jh in range(HALVES):
+            for t in every:
+                probe_passes(1, True, (jh,), (t,))
+                for a in range(K_PASSES):
+                    lot_passes(a, 1, False, (jh,), (t,))
+            square(1, (jh,))
+            if jh == 0:
+                quantize_h(0, 0, 512)
+        quantize_h(0, 512, 512)
+        quantize_wo(0, (0, 512))
+        quantize_h(1, 0, 256)
+        quantize_h(1, 256, 256)
+        quantize_wo(1, (1, 256))
+        readings(0, 512)
         quantize_h(1, 512, 256)
-        readings(512, 256, [(h_q[0, 512], 0), (h_q[1, 512], 0)])
+        readings(512, 256)
         quantize_h(1, 768, 256)
-        readings(768, 256, [(h_q[0, 768], 0), (h_q[1, 768], 0)])
+        readings(768, 256)

@@ -50,7 +50,7 @@ def tile_list_drum_curve_deviation_kernel(
             nc.vector.memset(plane[:].bitcast(I32), 0)
 
         def load_table_scales(q):
-            nc.sync.dma_start(
+            nc.gpsimd.dma_start(
                 out=tab_sc[32 * q : 32 * q + 4 * K_PASSES, :].bitcast(I32),
                 in_=tab_scales[:, 4 * q : 4 * q + 4, :].bitcast(I32),
             )
@@ -89,6 +89,8 @@ def tile_list_drum_curve_deviation_kernel(
         wb_raw = held([P, 2 * H], U8, "wb_raw")
         xs_sb = held([P, S], U32, "xs_sb")
 
+        for q in range(4):
+            load_table_scales(q)
         nc.sync.dma_start(offsets[:], offs)
         load_tab(0)
         for b in range(R_PASSES):
@@ -100,15 +102,13 @@ def tile_list_drum_curve_deviation_kernel(
         nc.sync.dma_start(out=wb_raw[:].bitcast(I32), in_=wb_words[0].bitcast(I32))
         nc.sync.dma_start(out=xs_sb[:].bitcast(I32), in_=xs_words[0].rearrange("p n i -> p (n i)").bitcast(I32))
         load_wa(0, 0, R_PASSES, 0)
-        for q in range(4):
-            load_table_scales(q)
         load_tab(1)
         for q in range(4):
             load_scale_rows(wb_sc_raw, wb_scales, q)
         load_wa(1, 0, 1, 1)
+        load_tab(2)
         for q in range(4):
             load_scale_rows(xs_sc, xs_scales, q)
-        load_tab(2)
         load_wa(2, 0, 1, 2)
         load_wa(1, 1, 1, 3)
         load_wa(2, 1, 1, 4)
@@ -207,9 +207,9 @@ def tile_list_drum_curve_deviation_kernel(
             woven = ring.tile([P, PACK * BANK], BF16, name="h_woven", align_bytes=64)
             first = j0 % BANK
             nc.vector.tensor_tensor(
-                woven[:, : PACK * width].rearrange("p (c i t) -> p c t i", i=4, t=PACK),
-                squares[b, j0 // BANK][:, :, first : first + width].rearrange("p t (c i) -> p c t i", i=4),
-                trust_sb[b, j0][:].rearrange("p t (c i) -> p c t i", i=4),
+                woven[:, : PACK * width].rearrange("p (c i t) -> p c t i", i=2, t=PACK),
+                squares[b, j0 // BANK][:, :, first : first + width].rearrange("p t (c i) -> p c t i", i=2),
+                trust_sb[b, j0][:].rearrange("p t (c i) -> p c t i", i=2),
                 MULT,
             )
             codes, scales = h_q[b, j0 // BANK]

@@ -1,6 +1,7 @@
 from contextlib import ExitStack
 
 import concourse.mybir as mybir
+from concourse.masks import make_identity
 
 K, K2, H, N, T, S = 1536, 512, 1024, 384, 4096, 1024
 FLOPS = 2 * S * (K * H + K2 * H + H * N)
@@ -91,14 +92,21 @@ def tile_list_drum_curve_deviation_kernel(
 
         for q in range(4):
             load_table_scales(q)
+        level_rows = held([P, P], F32, "level_rows")
+        identity = held([P, P], F32, "identity")
+        nc.gpsimd.memset(level_rows[:], 0.0)
+        nc.gpsimd.dma_start(out=level_rows[:N_TILES, :], in_=level.rearrange("(c p) -> c p", p=P))
+        make_identity(nc, identity[:])
+        turned = psum.tile([P, BANK], F32, name="bank")
+        nc.tensor.transpose(turned[:, :P], level_rows[:], identity[:])
+        nc.scalar.copy(level_sb[:], turned[:, :N_TILES])
+
         nc.sync.dma_start(offsets[:], offs)
         load_tab(0)
         for b in range(R_PASSES):
             nc.sync.dma_start(
                 out=lag_sb[b][:], in_=lag[PASS * b : PASS * (b + 1)].rearrange("(p t) -> p t", t=PACK)
             )
-        with nc.allow_non_contiguous_dma(reason="one bias value a partition"):
-            nc.sync.dma_start(out=level_sb[:], in_=level.rearrange("(c p) -> p c", p=P))
         nc.sync.dma_start(out=wb_raw[:].bitcast(I32), in_=wb_words[0].bitcast(I32))
         nc.sync.dma_start(out=xs_sb[:].bitcast(I32), in_=xs_words[0].rearrange("p n i -> p (n i)").bitcast(I32))
         load_wa(0, 0, R_PASSES, 0)
@@ -114,10 +122,11 @@ def tile_list_drum_curve_deviation_kernel(
         load_wa(2, 1, 1, 4)
         load_trust(0, 0, 512)
         load_wo(0)
-        load_trust(0, 512, 512)
+        load_trust(1, 0, 512)
         load_wo(1)
-        for j0 in range(0, S, 256):
-            load_trust(1, j0, 256)
+        for j0 in (512, 768):
+            for b in range(R_PASSES):
+                load_trust(b, j0, 256)
 
         picked, wa_q, acc, squares, wo_q, h_q = {}, {}, {}, {}, {}, {}
         for b in range(R_PASSES):
@@ -281,13 +290,13 @@ def tile_list_drum_curve_deviation_kernel(
             square(1, (jh,))
             if jh == 0:
                 quantize_h(0, 0, 512)
-        quantize_h(0, 512, 512)
-        quantize_wo(0, (0, 512))
-        quantize_h(1, 0, 256)
-        quantize_h(1, 256, 256)
-        quantize_wo(1, (1, 256))
+        quantize_h(1, 0, 512)
+        quantize_wo(0, (1, 0))
+        quantize_h(0, 512, 256)
+        quantize_wo(1, (0, 512))
         readings(0, 512)
         quantize_h(1, 512, 256)
         readings(512, 256)
+        quantize_h(0, 768, 256)
         quantize_h(1, 768, 256)
         readings(768, 256)

from contextlib import ExitStack

import concourse.mybir as mybir
from concourse.masks import make_identity

K, K2, H, N, T, S = 1536, 512, 1024, 384, 4096, 1024
FLOPS = 2 * S * (K * H + K2 * H + H * N)

F32 = mybir.dt.float32
BF16 = mybir.dt.bfloat16
I32 = mybir.dt.int32
U32 = mybir.dt.uint32
U16 = mybir.dt.uint16
U8 = mybir.dt.uint8
FP8X4 = mybir.dt.float8_e4m3fn_x4
FP4X4 = mybir.dt.float4_e2m1fn_x4
ACT = mybir.ActivationFunctionType
MULT = mybir.AluOpType.mult

P = 128
PACK = 4
PASS = P * PACK
BANK = 512
K_PASSES = K // PASS
R_PASSES = H // PASS
HALVES = S // BANK
N_TILES = N // P


def tile_list_drum_curve_deviation_kernel(
    tc, tab_words, tab_scales, offs, xs_words, xs_scales, wa, wb_words, wb_scales, lag, trust, wo, level, out
):
    nc = tc.nc
    with ExitStack() as ctx:
        keep = ctx.enter_context(tc.tile_pool(name="keep", bufs=1))
        ring = ctx.enter_context(tc.tile_pool(name="ring", bufs=2))
        psum = ctx.enter_context(tc.psum_pool(name="psum", bufs=8))

        def held(shape, dtype, name, tag=None):
            return keep.tile(shape, dtype, name=name, tag=tag or name, align_bytes=64)

        offsets = keep.tile([P, S // 16], U16, name="offsets")
        tab_sc = held([P, T], U8, "tab_sc")
        wb_sc_raw = held([P, H], U8, "wb_sc_raw")
        xs_sc = held([P, S], U8, "xs_sc")
        lag_sb = [held([P, PACK], F32, "lag_sb_%d" % b) for b in range(R_PASSES)]
        level_sb = held([P, N_TILES], F32, "level_sb")

        nc.gpsimd.memset(tab_sc[:].bitcast(I32), 0)
        for plane in (wb_sc_raw, xs_sc):
            nc.vector.memset(plane[:].bitcast(I32), 0)

        def load_table_scales(q):
            nc.gpsimd.dma_start(
                out=tab_sc[32 * q : 32 * q + 4 * K_PASSES, :].bitcast(I32),
                in_=tab_scales[:, 4 * q : 4 * q + 4, :].bitcast(I32),
            )

        def load_scale_rows(plane, rows, q):
            nc.sync.dma_start(
                out=plane[32 * q : 32 * q + 4, :].bitcast(I32),
                in_=rows[0, 4 * q : 4 * q + 4, :].bitcast(I32),
            )

        tab_sb, wa_raw, trust_sb, wo_raw = {}, {}, {}, {}

        def load_tab(a):
            tab_sb[a] = held([P, T], U32, "tab_%d" % a)
            nc.sync.dma_start(
                out=tab_sb[a][:].bitcast(I32), in_=tab_words[a].rearrange("p n i -> p (n i)").bitcast(I32)
            )

        def load_wa(a, first, count, slot):
            raw = keep.tile([P, PACK, PASS * count], F32, name="wa_raw_%d_%d" % (a, first), tag="slot_%d" % slot)
            rows = wa[PASS * a : PASS * (a + 1), PASS * first : PASS * (first + count)]
            nc.sync.dma_start(out=raw[:], in_=rows.rearrange("(p i) r -> p i r", i=PACK))
            for b in range(count):
                wa_raw[a, first + b] = raw[:, :, PASS * b : PASS * (b + 1)]

        def load_trust(b, j0, width):
            trust_sb[b, j0] = held([P, PACK, width], F32, "trust_%d_%d" % (b, j0))
            rows = trust[PASS * b : PASS * (b + 1), j0 : j0 + width]
            nc.sync.dma_start(out=trust_sb[b, j0][:], in_=rows.rearrange("(p t) j -> p t j", t=PACK))

        def load_wo(b):
            wo_raw[b] = held([P, PACK, N], F32, "wo_raw_%d" % b)
            rows = wo[PASS * b : PASS * (b + 1), :]
            nc.sync.dma_start(out=wo_raw[b][:], in_=rows.rearrange("(p t) n -> p t n", t=PACK))

        wb_raw = held([P, 2 * H], U8, "wb_raw")
        xs_sb = held([P, S], U32, "xs_sb")

        for q in range(4):
            load_table_scales(q)
        level_rows = held([P, P], F32, "level_rows")
        identity = held([P, P], F32, "identity")
        nc.gpsimd.memset(level_rows[:], 0.0)
        nc.gpsimd.dma_start(out=level_rows[:N_TILES, :], in_=level.rearrange("(c p) -> c p", p=P))
        make_identity(nc, identity[:])
        turned = psum.tile([P, BANK], F32, name="bank")
        nc.tensor.transpose(turned[:, :P], level_rows[:], identity[:])
        nc.scalar.copy(level_sb[:], turned[:, :N_TILES])

        nc.sync.dma_start(offsets[:], offs)
        load_tab(0)
        for b in range(R_PASSES):
            nc.sync.dma_start(
                out=lag_sb[b][:], in_=lag[PASS * b : PASS * (b + 1)].rearrange("(p t) -> p t", t=PACK)
            )
        nc.sync.dma_start(out=wb_raw[:].bitcast(I32), in_=wb_words[0].bitcast(I32))
        nc.sync.dma_start(out=xs_sb[:].bitcast(I32), in_=xs_words[0].rearrange("p n i -> p (n i)").bitcast(I32))
        load_wa(0, 0, R_PASSES, 0)
        load_tab(1)
        for q in range(4):
            load_scale_rows(wb_sc_raw, wb_scales, q)
        load_wa(1, 0, 1, 1)
        load_tab(2)
        for q in range(4):
            load_scale_rows(xs_sc, xs_scales, q)
        load_wa(2, 0, 1, 2)
        load_wa(1, 1, 1, 3)
        load_wa(2, 1, 1, 4)
        load_trust(0, 0, 512)
        load_wo(0)
        load_trust(1, 0, 512)
        load_wo(1)
        for j0 in (512, 768):
            for b in range(R_PASSES):
                load_trust(b, j0, 256)

        picked, wa_q, acc, squares, wo_q, h_q = {}, {}, {}, {}, {}, {}
        for b in range(R_PASSES):
            for jh in range(HALVES):
                h_q[b, jh] = (
                    held([P, BANK], U32, "h_codes_%d_%d" % (b, jh)),
                    held([P, BANK], U8, "h_scales_%d_%d" % (b, jh)),
                )
        picked_sc = held([P, S], U8, "picked_sc")
        wb_q = held([P, 2 * H], U8, "wb_q")
        wb_sc = held([P, H], U8, "wb_sc")

        def gather_words(a):
            for jh in range(HALVES):
                picked[a, jh] = held([P, BANK], U32, "picked_%d_%d" % (a, jh))
                cols = slice(jh * BANK // 16, (jh + 1) * BANK // 16)
                nc.vector.tensor_copy(picked[a, jh][:], tab_sb[a][:].indirect(offsets[:, cols]))

        def quantize(flat, words, name, tag=None):
            codes = held([P, words], U32, name + "_codes", tag)
            scales = held([P, words], U8, name + "_scales")
            done = 0
            while done < words:
                step = 512 if words - done >= 512 else (256 if words - done >= 256 else 128)
                nc.vector.quantize_mx(
                    out=codes[:, done : done + step].bitcast(FP8X4),
                    scales=scales[:, done : done + step],
                    in_=flat[:, PACK * done : PACK * (done + step)],
                )
                done = done + step
            return codes, scales

        def quantize_wa(a, b, on_scalar):
            woven = ring.tile([P, PACK * BANK], BF16, name="wa_woven", align_bytes=64)
            dst = woven[:].rearrange("p (t m i) -> p m i t", t=PACK, i=PACK)
            src = wa_raw[a, b].rearrange("p i (m t) -> p m i t", t=PACK)
            if on_scalar:
                nc.scalar.activation(dst, src, ACT.Copy, scale=-1.0)
            else:
                nc.vector.tensor_scalar_mul(dst, src, -1.0)
            wa_q[a, b] = quantize(woven, BANK, "wa_%d_%d" % (a, b))

        def open_banks(b):
            for jh in range(HALVES):
                for t in range(PACK):
                    acc[b, jh, t] = psum.tile([P, BANK], F32, name="bank")

        def probe_passes(b, start, halves, tiles):
            for jh in halves:
                for t in tiles:
                    col = PASS * b + P * t
                    nc.tensor.matmul_mx(
                        out=acc[b, jh, t][:],
                        lhsT=wb_q[:, 2 * col : 2 * (col + P)].bitcast(FP4X4),
                        lhsT_scale=wb_sc[:, col : col + P],
                        rhs=xs_sb[:, BANK * jh : BANK * (jh + 1)].bitcast(FP8X4),
                        rhs_scale=xs_sc[:, BANK * jh : BANK * (jh + 1)],
                        start=start,
                        stop=False,
                    )

        def lot_passes(a, b, start, halves, tiles):
            codes, scales = wa_q[a, b]
            for jh in halves:
                for t in tiles:
                    nc.tensor.matmul_mx(
                        out=acc[b, jh, t][:],
                        lhsT=codes[:, P * t : P * (t + 1)].bitcast(FP8X4),
                        lhsT_scale=scales[:, P * t : P * (t + 1)],
                        rhs=picked[a, jh][:].bitcast(FP8X4),
                        rhs_scale=picked_sc[4 * a : P, BANK * jh : BANK * (jh + 1)],
                        start=start,
                        stop=(a == K_PASSES - 1),
                    )

        def square(b, halves):
            for jh in halves:
                squares[b, jh] = keep.tile(
                    [P, PACK, BANK], F32, name="squares_%d_%d" % (b, jh), tag="slot_%d" % (HALVES * b + jh)
                )
                for t in range(PACK):
                    nc.scalar.activation(
                        squares[b, jh][:, t, :], acc[b, jh, t][:], ACT.Square, bias=lag_sb[b][:, t : t + 1]
                    )

        def quantize_h(b, j0, width):
            woven = ring.tile([P, PACK * BANK], BF16, name="h_woven", align_bytes=64)
            first = j0 % BANK
            nc.vector.tensor_tensor(
                woven[:, : PACK * width].rearrange("p (c i t) -> p c t i", i=2, t=PACK),
                squares[b, j0 // BANK][:, :, first : first + width].rearrange("p t (c i) -> p c t i", i=2),
                trust_sb[b, j0][:].rearrange("p t (c i) -> p c t i", i=2),
                MULT,
            )
            codes, scales = h_q[b, j0 // BANK]
            nc.vector.quantize_mx(
                out=codes[:, first : first + width].bitcast(FP8X4),
                scales=scales[:, first : first + width],
                in_=woven[:, : PACK * width],
            )

        def quantize_wo(b, after):
            woven = held([P, PACK * N], BF16, "wo_woven_%d" % b)
            nc.scalar.copy(
                woven[:].rearrange("p (c i t) -> p c t i", i=4, t=PACK),
                wo_raw[b][:].rearrange("p t (c i) -> p c t i", i=4),
            )
            wo_q[b] = quantize(woven, N, "wo_%d" % b, "trust_%d_%d" % after)

        def readings(j0, width):
            first = j0 % BANK
            for c in range(N_TILES):
                bank = psum.tile([P, BANK], F32, name="bank")
                for b in range(R_PASSES):
                    w_codes, w_scales = wo_q[b]
                    h_codes, h_scales = h_q[b, j0 // BANK]
                    nc.tensor.matmul_mx(
                        out=bank[:, :width],
                        lhsT=w_codes[:, P * c : P * (c + 1)].bitcast(FP8X4),
                        lhsT_scale=w_scales[:, P * c : P * (c + 1)],
                        rhs=h_codes[:, first : first + width].bitcast(FP8X4),
                        rhs_scale=h_scales[:, first : first + width],
                        start=(b == 0),
                        stop=(b == R_PASSES - 1),
                    )
                result = held([P, width], F32, "result_%d_%d" % (j0, c))
                nc.scalar.activation(result[:], bank[:, :width], ACT.Tanh, bias=level_sb[:, c : c + 1])
                nc.sync.dma_start(out=out[P * c : P * (c + 1), j0 : j0 + width], in_=result[:])

        gather_words(0)
        nc.vector.tensor_copy(picked_sc[:], tab_sc[:].indirect(offsets[:]))
        nc.vector.tensor_copy(
            wb_q[:].rearrange("p (b t m c) -> p b t m c", t=PACK, m=P, c=2),
            wb_raw[:].rearrange("p (b m t c) -> p b t m c", t=PACK, m=P, c=2),
        )
        every = range(PACK)
        quantize_wa(0, 0, True)
        open_banks(0)
        lot_passes(0, 0, True, (0, 1), every)
        quantize_wa(0, 1, True)
        gather_words(1)
        nc.vector.tensor_copy(
            wb_sc[:].rearrange("p (b t m) -> p b t m", t=PACK, m=P),
            wb_sc_raw[:].rearrange("p (b m t) -> p b t m", t=PACK, m=P),
        )
        quantize_wa(1, 0, True)
        lot_passes(1, 0, False, (0, 1), every)
        probe_passes(0, False, (0, 1), every)
        gather_words(2)
        quantize_wa(2, 0, False)
        lot_passes(2, 0, False, (0, 1), every)
        square(0, (0, 1))
        quantize_wa(1, 1, False)
        quantize_wa(2, 1, False)
        open_banks(1)
        for jh in range(HALVES):
            for t in every:
                probe_passes(1, True, (jh,), (t,))
                for a in range(K_PASSES):
                    lot_passes(a, 1, False, (jh,), (t,))
            square(1, (jh,))
            if jh == 0:
                quantize_h(0, 0, 512)
        quantize_h(1, 0, 512)
        quantize_wo(0, (1, 0))
        quantize_h(0, 512, 256)
        quantize_wo(1, (0, 512))
        readings(0, 512)
        quantize_h(1, 512, 256)
        readings(512, 256)
        quantize_h(0, 768, 256)
        quantize_h(1, 768, 256)
        readings(768, 256)
